import numpy as np
import ml_dtypes


def mxq(x, axis, fmt="e4m3"):
    dtype, down = {"e4m3": (ml_dtypes.float8_e4m3fn, 7), "e5m2": (ml_dtypes.float8_e5m2, 14)}[fmt]
    v = np.moveaxis(np.asarray(x, np.float32).astype(ml_dtypes.bfloat16).astype(np.float64), axis, -1)
    blocks = v.reshape(v.shape[:-1] + (-1, 32))
    amax = np.abs(blocks).max(-1, keepdims=True)
    byte = np.maximum(np.where(amax > 0, np.frexp(amax)[1] - 1 + 127, 0) - down, 1)
    scale = np.exp2(byte - 127.0)
    codes = (blocks / scale).astype(np.float32).astype(dtype).astype(np.float64)
    return np.moveaxis((codes * scale).reshape(v.shape), -1, axis)


WIDE = False


def mx_kscale(k):
    if not WIDE:
        return np.ones(k)
    levels = np.array([10, -10, 5, -5, 0])
    if k % 512:
        return np.exp2(np.random.permutation(np.resize(levels, k // 32))).repeat(32)
    a = np.empty((k // 512, 16))
    for p in range(k // 512):
        a[p, :8] = np.random.permutation(np.resize(levels, 8))
        for g in range(8):
            far = levels[np.abs(levels - a[p, g]) >= 10]
            a[p, g + 8] = far[np.random.randint(len(far))]
    return np.exp2(a.ravel()).repeat(32)


def f64(x):
    return np.asarray(x).astype(np.float64)


def striped(idx):
    return np.tile(idx.reshape(-1, 16).T, (8, 1)).astype(np.uint16)


def unstriped(offs):
    return offs[:16].T.reshape(-1).astype(np.int64)


def striped8(idx):
    return np.concatenate([x.reshape(-1, 16).T for x in idx]).astype(np.uint16)


def runs(offs, k):
    lists = np.stack([offs[16 * r : 16 * r + 16].T.reshape(-1) for r in range(8)]).astype(np.int64)
    return lists[np.arange(k) % 512 // 64]


def pack_weight(w):
    k, n = w.shape
    w = f64(np.asarray(w, np.float32).astype(ml_dtypes.bfloat16)).reshape(k // 32, 32, n)
    amax = np.abs(w).max(1)
    byte = np.clip(np.where(amax > 0, np.frexp(amax)[1] - 1 + 127 - 7, 1), 1, 254)
    scaled = (w * np.exp2(127.0 - byte)[:, None, :]).reshape(k, n).astype(np.float32)
    words = np.ascontiguousarray(scaled.reshape(k // 512, 128, 4, n).transpose(0, 1, 3, 2)).astype(ml_dtypes.float8_e4m3fn).view(np.uint8)
    return words, np.ascontiguousarray(byte.astype(np.uint8).reshape(k // 512, 16, n))


def unpack_weight(words, scales):
    g, p, n, _ = words.shape
    vals = np.ascontiguousarray(words).view(ml_dtypes.float8_e4m3fn).astype(np.float64) * np.repeat(np.exp2(scales.astype(np.float64) - 127.0), 8, axis=1)[..., None]
    return vals.transpose(0, 1, 3, 2).reshape(g * 512, n)


K, T, S, V, H, C = 512, 2048, 1024, 512, 512, 512


def setup_inputs():
    n = np.random.standard_normal
    s = mx_kscale(K)[:, None]
    packed_xT = pack_weight(n((K, T)) * s)
    return {
        "x_words": packed_xT[0],
        "x_scales": packed_xT[1],
        "w1": (n((K, H)) / np.sqrt(K) / s).astype(np.float32),
        "gs": (np.random.uniform(0.5, 1.5, (K, 1)) / s).astype(np.float32),
        "offs": striped(np.random.permutation(T)[:S]),
        "order": striped8(np.stack([np.random.permutation(S) for _ in range(8)])),
        "cand": striped(np.random.permutation(T)[:C]),
    }


def reference(x_words, x_scales, w1, gs, offs, order, cand):
    x_cand = unpack_weight(x_words, x_scales)[:, unstriped(cand)]
    xq = unpack_weight(x_words, x_scales)[:, unstriped(offs)]
    h = mxq(f64(w1), 0, "e4m3").T @ xq
    o = h[np.arange(H)[:, None], runs(order, H)]
    mx = o.reshape(H, V, 2).max(axis=2)
    mn = o.reshape(H, V, 2).min(axis=2)
    z = f64(gs) * (mx - (0.5 * mn))
    return 0.0625 * ((x_cand.T @ mxq(z, 0, "e4m3")))

@@ -1,0 +1,202 @@
+from contextlib import ExitStack
+
+import concourse.mybir as mybir
+
+K, T, S, V, H, C = 512, 2048, 1024, 512, 512, 512
+FLOPS = 2 * K * H * S + 2 * K * C * V
+
+F32 = mybir.dt.float32
+BF16 = mybir.dt.bfloat16
+I32 = mybir.dt.int32
+U32 = mybir.dt.uint32
+U16 = mybir.dt.uint16
+U8 = mybir.dt.uint8
+FP8X4 = mybir.dt.float8_e4m3fn_x4
+ALU = mybir.AluOpType
+COPY = mybir.ActivationFunctionType.Copy
+
+P = 128
+PACK = 4
+BANK = 512
+HALF_V = V // 2
+
+
+def tile_picked_candwide_none_p_kernel(
+    tc, x_words, x_scales, w1, gs, offs, order, cand, out
+):
+    nc = tc.nc
+    with ExitStack() as ctx:
+        keep = ctx.enter_context(tc.tile_pool(name="keep", bufs=1))
+        psum = ctx.enter_context(tc.psum_pool(name="psum", bufs=8))
+
+        offs_t = keep.tile([P, S // 16], U16, name="offs_t")
+        order_t = keep.tile([P, S // 16], U16, name="order_t")
+        cand_t = keep.tile([P, C // 16], U16, name="cand_t")
+        word_table = keep.tile([P, T], I32, name="word_table", align_bytes=64)
+        byte_table = keep.tile([P, T], U8, name="byte_table", align_bytes=64)
+        gain = keep.tile([P, PACK], F32, name="gain")
+
+        nc.gpsimd.memset(byte_table[:].bitcast(I32), 0)
+        nc.sync.dma_start(offs_t[:], offs)
+        for q in range(4):
+            nc.scalar.dma_start(
+                byte_table[32 * q : 32 * q + 4, :].bitcast(I32), x_scales[0, 4 * q : 4 * q + 4, :].bitcast(I32)
+            )
+        w_rows = w1.rearrange("(p j) c -> p j c", j=PACK)
+        w_raw = []
+        for u in range(2):
+            raw = keep.tile([P, PACK, H // 2], F32, name="w_raw%d" % u)
+            nc.sync.dma_start(raw[:], w_rows[:, :, u * (H // 2) : (u + 1) * (H // 2)])
+            w_raw.append(raw)
+        nc.sync.dma_start(word_table[:], x_words[0].rearrange("p n t -> p (n t)").bitcast(I32))
+        nc.gpsimd.dma_start(gain[:], gs.rearrange("(p t) o -> p (t o)", t=PACK))
+        nc.sync.dma_start(cand_t[:], cand)
+        nc.sync.dma_start(order_t[:], order)
+
+        x_bytes, x_codes = [], []
+        for c in range(2):
+            picked = keep.tile([P, BANK], U8, name="x_bytes%d" % c, align_bytes=64)
+            nc.vector.tensor_copy(picked[:], byte_table[:].indirect(offs_t[:, 32 * c : 32 * c + 32]))
+            x_bytes.append(picked)
+
+        def pick_words(c):
+            picked = keep.tile([P, BANK], U32, name="x_codes%d" % c, align_bytes=64)
+            nc.vector.tensor_copy(picked[:], word_table[:].bitcast(U32).indirect(offs_t[:, 32 * c : 32 * c + 32]))
+            x_codes.append(picked)
+
+        w_bf = keep.tile([P, PACK * P * PACK], BF16, name="w_bf", align_bytes=64)
+        w_bf_view = w_bf[:].rearrange("p (t m j) -> p m j t", t=PACK, j=PACK)
+        for u in range(2):
+            nc.scalar.copy(
+                w_bf_view[:, 64 * u : 64 * u + 64], w_raw[u][:].rearrange("p j (m t) -> p m j t", t=PACK)
+            )
+        w_codes = keep.tile([P, PACK * P], U32, name="w_codes", align_bytes=64)
+        w_bytes = keep.tile([P, PACK * P], U8, name="w_bytes", align_bytes=64)
+        nc.vector.quantize_mx(out=w_codes[:].bitcast(FP8X4), scales=w_bytes[:], in_=w_bf[:])
+        pick_words(0)
+        pick_words(1)
+
+        half_gain = keep.tile([P, PACK], F32, name="half_gain")
+        positive = keep.tile([P, PACK], F32, name="positive")
+        slope = keep.tile([P, PACK], F32, name="slope")
+        weight = keep.tile([P, PACK], F32, name="weight")
+        nc.gpsimd.tensor_scalar(half_gain[:], gain[:], 0.5, None, ALU.mult)
+        nc.gpsimd.tensor_scalar(positive[:], gain[:], 0.0, None, ALU.is_ge)
+        nc.gpsimd.tensor_scalar(slope[:], positive[:], 1.5, -2.0, ALU.mult, ALU.add)
+        nc.gpsimd.tensor_scalar(weight[:], positive[:], 3.0, -1.0, ALU.mult, ALU.add)
+
+        cand_bytes = keep.tile([P, C], U8, name="cand_bytes", align_bytes=64)
+        cand_codes = keep.tile([P, C], U32, name="cand_codes", align_bytes=64)
+
+        h_rows = []
+
+        def first_product(t):
+            rows = keep.tile([P, S], F32, name="h_rows%d" % t)
+            cols = slice(t * P, (t + 1) * P)
+            for c in range(2):
+                bank = psum.tile([P, BANK], F32, name="bank")
+                nc.tensor.matmul_mx(
+                    out=bank[:],
+                    lhsT=w_codes[:, cols].bitcast(FP8X4),
+                    lhsT_scale=w_bytes[:, cols],
+                    rhs=x_codes[c][:].bitcast(FP8X4),
+                    rhs_scale=x_bytes[c][:],
+                    start=True,
+                    stop=True,
+                )
+                nc.scalar.activation(rows[:, c * BANK : (c + 1) * BANK], bank[:], COPY, scale=half_gain[:, t : t + 1])
+            h_rows.append(rows)
+
+        lined, pair_tiles = {}, {}
+
+        def look_up(t, u, on_vector):
+            if (t // 2, u) not in pair_tiles:
+                pair_tiles[t // 2, u] = keep.tile([P, 4 * HALF_V], F32, name="lined%d_%d" % (t // 2, u))
+            got = pair_tiles[t // 2, u][:, (t % 2) * 2 * HALF_V : (t % 2 + 1) * 2 * HALF_V]
+            window = h_rows[t][:].indirect(order_t[:, 32 * u : 32 * u + 32])
+            if on_vector:
+                nc.vector.tensor_copy(got, window)
+            else:
+                nc.scalar.activation(got, window, COPY)
+            lined[t, u] = got
+
+        z_rows = [keep.tile([P, PACK * HALF_V], BF16, name="z_rows%d" % u) for u in range(2)]
+
+        def contrast(ts, u):
+            diff, bent = {}, {}
+            both = keep.tile([P, len(ts) * HALF_V], F32, name="diff%d_%d" % (ts[0], u))
+            source = lined[ts[0], u] if len(ts) == 1 else pair_tiles[ts[0] // 2, u][:]
+            pairs = source.rearrange("p (v two) -> p v two", two=2)
+            nc.vector.tensor_tensor(both[:], pairs[:, :, 0], pairs[:, :, 1], ALU.subtract)
+            for n, t in enumerate(ts):
+                diff[t] = both[:, n * HALF_V : (n + 1) * HALF_V]
+            for t in ts:
+                bent[t] = keep.tile([P, HALF_V], F32, name="bent%d_%d" % (t, u))
+                nc.vector.scalar_tensor_tensor(
+                    bent[t][:], diff[t], slope[:, t : t + 1], diff[t], ALU.mult, ALU.max
+                )
+            for t in ts:
+                pairs = lined[t, u].rearrange("p (v two) -> p v two", two=2)
+                nc.vector.scalar_tensor_tensor(
+                    z_rows[u][:, t * HALF_V : (t + 1) * HALF_V],
+                    bent[t][:],
+                    weight[:, t : t + 1],
+                    pairs[:, :, 1],
+                    ALU.mult,
+                    ALU.add,
+                )
+
+        out_rows = out.rearrange("(b p) v -> p b v", p=P)
+
+        def second_product(u):
+            woven = keep.tile([P, HALF_V * PACK], BF16, name="z_woven%d" % u, align_bytes=64)
+            nc.vector.tensor_copy(
+                woven[:].rearrange("p (c i t) -> p c t i", i=4, t=PACK),
+                z_rows[u][:].rearrange("p (t c i) -> p c t i", i=4, t=PACK),
+            )
+            z_codes = keep.tile([P, HALF_V], U32, name="z_codes%d" % u, align_bytes=64)
+            z_bytes = keep.tile([P, HALF_V], U8, name="z_bytes%d" % u, align_bytes=64)
+            nc.vector.quantize_mx(out=z_codes[:].bitcast(FP8X4), scales=z_bytes[:], in_=woven[:])
+            for g in range(2):
+                bank = psum.tile([P, BANK], F32, name="bank")
+                for b in range(2):
+                    cols = slice((2 * g + b) * P, (2 * g + b + 1) * P)
+                    nc.tensor.matmul_mx(
+                        out=bank[:, b * HALF_V : (b + 1) * HALF_V],
+                        lhsT=cand_codes[:, cols].bitcast(FP8X4),
+                        lhsT_scale=cand_bytes[:, cols],
+                        rhs=z_codes[:].bitcast(FP8X4),
+                        rhs_scale=z_bytes[:],
+                        start=True,
+                        stop=True,
+                    )
+                scores = keep.tile([P, BANK], F32, name="scores%d_%d" % (u, g))
+                if u == 1 and g == 1:
+                    nc.vector.tensor_scalar(scores[:], bank[:], 0.0625, None, ALU.mult)
+                else:
+                    nc.scalar.activation(scores[:], bank[:], COPY, scale=0.0625)
+                nc.sync.dma_start(
+                    out_rows[:, 2 * g : 2 * g + 2, u * HALF_V : (u + 1) * HALF_V],
+                    scores[:].rearrange("p (b v) -> p b v", b=2),
+                )
+
+        first_product(0)
+        first_product(1)
+        look_up(0, 0, True)
+        nc.vector.tensor_copy(cand_bytes[:], byte_table[:].indirect(cand_t[:]))
+        look_up(1, 0, False)
+        first_product(2)
+        contrast([0, 1], 0)
+        nc.vector.tensor_copy(cand_codes[:], word_table[:].bitcast(U32).indirect(cand_t[:]))
+        look_up(2, 0, False)
+        first_product(3)
+        look_up(0, 1, True)
+        look_up(3, 0, False)
+        contrast([2, 3], 0)
+        look_up(1, 1, False)
+        look_up(2, 1, False)
+        look_up(3, 1, False)
+        second_product(0)
+        contrast([0, 1], 1)
+        contrast([2, 3], 1)
+        second_product(1)

@@ -38,6 +38,9 @@ def tile_picked_candwide_none_p_kernel(
 
         nc.gpsimd.memset(byte_table[:].bitcast(I32), 0)
         nc.sync.dma_start(offs_t[:], offs)
+        nc.sync.dma_start(cand_t[:], cand)
+        nc.sync.dma_start(order_t[:], order)
+        nc.sync.dma_start(word_table[:], x_words[0].rearrange("p n t -> p (n t)").bitcast(I32))
         for q in range(4):
             nc.scalar.dma_start(
                 byte_table[32 * q : 32 * q + 4, :].bitcast(I32), x_scales[0, 4 * q : 4 * q + 4, :].bitcast(I32)
@@ -48,14 +51,16 @@ def tile_picked_candwide_none_p_kernel(
             raw = keep.tile([P, PACK, H // 2], F32, name="w_raw%d" % u)
             nc.sync.dma_start(raw[:], w_rows[:, :, u * (H // 2) : (u + 1) * (H // 2)])
             w_raw.append(raw)
-        nc.sync.dma_start(word_table[:], x_words[0].rearrange("p n t -> p (n t)").bitcast(I32))
-        nc.gpsimd.dma_start(gain[:], gs.rearrange("(p t) o -> p (t o)", t=PACK))
-        nc.sync.dma_start(cand_t[:], cand)
-        nc.sync.dma_start(order_t[:], order)
+        nc.sync.dma_start(gain[:], gs.rearrange("(p t) o -> p (t o)", t=PACK))
 
         x_bytes, x_codes = [], []
-        for c in range(2):
-            picked = keep.tile([P, BANK], U8, name="x_bytes%d" % c, align_bytes=64)
+        shared = ctx.enter_context(tc.tile_pool(name="shared", bufs=1))
+
+        def pick_bytes(c):
+            if c == 0:
+                picked = keep.tile([P, BANK], U8, name="x_bytes0", align_bytes=64)
+            else:
+                picked = shared.tile([P, BANK], U8, name="x_bytes1", align_bytes=64, offset=512)
             nc.vector.tensor_copy(picked[:], byte_table[:].indirect(offs_t[:, 32 * c : 32 * c + 32]))
             x_bytes.append(picked)
 
@@ -64,7 +69,11 @@ def tile_picked_candwide_none_p_kernel(
             nc.vector.tensor_copy(picked[:], word_table[:].bitcast(U32).indirect(offs_t[:, 32 * c : 32 * c + 32]))
             x_codes.append(picked)
 
-        w_bf = keep.tile([P, PACK * P * PACK], BF16, name="w_bf", align_bytes=64)
+        pick_words(0)
+        pick_words(1)
+        pick_bytes(0)
+
+        w_bf = shared.tile([P, PACK * P * PACK], BF16, name="w_bf", align_bytes=64, offset=0)
         w_bf_view = w_bf[:].rearrange("p (t m j) -> p m j t", t=PACK, j=PACK)
         for u in range(2):
             nc.scalar.copy(
@@ -73,8 +82,7 @@ def tile_picked_candwide_none_p_kernel(
         w_codes = keep.tile([P, PACK * P], U32, name="w_codes", align_bytes=64)
         w_bytes = keep.tile([P, PACK * P], U8, name="w_bytes", align_bytes=64)
         nc.vector.quantize_mx(out=w_codes[:].bitcast(FP8X4), scales=w_bytes[:], in_=w_bf[:])
-        pick_words(0)
-        pick_words(1)
+        pick_bytes(1)
 
         half_gain = keep.tile([P, PACK], F32, name="half_gain")
         positive = keep.tile([P, PACK], F32, name="positive")
@@ -85,33 +93,37 @@ def tile_picked_candwide_none_p_kernel(
         nc.gpsimd.tensor_scalar(slope[:], positive[:], 1.5, -2.0, ALU.mult, ALU.add)
         nc.gpsimd.tensor_scalar(weight[:], positive[:], 3.0, -1.0, ALU.mult, ALU.add)
 
-        cand_bytes = keep.tile([P, C], U8, name="cand_bytes", align_bytes=64)
-        cand_codes = keep.tile([P, C], U32, name="cand_codes", align_bytes=64)
+        cand_bytes = shared.tile([P, C], U8, name="cand_bytes", align_bytes=64, offset=0)
+        cand_codes = shared.tile([P, C], U32, name="cand_codes", align_bytes=64, offset=1024)
 
-        h_rows = []
+        h_rows = [keep.tile([P, S], F32, name="h_rows%d" % t) for t in range(PACK)]
 
-        def first_product(t):
-            rows = keep.tile([P, S], F32, name="h_rows%d" % t)
+        def first_product(t, c):
             cols = slice(t * P, (t + 1) * P)
-            for c in range(2):
-                bank = psum.tile([P, BANK], F32, name="bank")
-                nc.tensor.matmul_mx(
-                    out=bank[:],
-                    lhsT=w_codes[:, cols].bitcast(FP8X4),
-                    lhsT_scale=w_bytes[:, cols],
-                    rhs=x_codes[c][:].bitcast(FP8X4),
-                    rhs_scale=x_bytes[c][:],
-                    start=True,
-                    stop=True,
+            bank = psum.tile([P, BANK], F32, name="bank")
+            nc.tensor.matmul_mx(
+                out=bank[:],
+                lhsT=w_codes[:, cols].bitcast(FP8X4),
+                lhsT_scale=w_bytes[:, cols],
+                rhs=x_codes[c][:].bitcast(FP8X4),
+                rhs_scale=x_bytes[c][:],
+                start=True,
+                stop=True,
+            )
+            if (t, c) == (3, 1):
+                nc.vector.tensor_scalar(
+                    h_rows[t][:, c * BANK : (c + 1) * BANK], bank[:], half_gain[:, t : t + 1], None, ALU.mult
                 )
-                nc.scalar.activation(rows[:, c * BANK : (c + 1) * BANK], bank[:], COPY, scale=half_gain[:, t : t + 1])
-            h_rows.append(rows)
+            else:
+                nc.scalar.activation(
+                    h_rows[t][:, c * BANK : (c + 1) * BANK], bank[:], COPY, scale=half_gain[:, t : t + 1]
+                )
 
         lined, pair_tiles = {}, {}
 
         def look_up(t, u, on_vector):
-            if (t // 2, u) not in pair_tiles:
-                pair_tiles[t // 2, u] = keep.tile([P, 4 * HALF_V], F32, name="lined%d_%d" % (t // 2, u))
+            if t % 2 == 0:
+                pair_tiles[t // 2, u] = keep.tile([P, 4 * HALF_V], F32, name="lined%d_%d" % (t, u))
             got = pair_tiles[t // 2, u][:, (t % 2) * 2 * HALF_V : (t % 2 + 1) * 2 * HALF_V]
             window = h_rows[t][:].indirect(order_t[:, 32 * u : 32 * u + 32])
             if on_vector:
@@ -148,21 +160,23 @@ def tile_picked_candwide_none_p_kernel(
 
         out_rows = out.rearrange("(b p) v -> p b v", p=P)
 
-        def second_product(u):
-            woven = keep.tile([P, HALF_V * PACK], BF16, name="z_woven%d" % u, align_bytes=64)
-            nc.vector.tensor_copy(
+        def second_product(u, start, width, engines, weave):
+            name = "%d_%d" % (u, start)
+            woven = keep.tile([P, width * PACK], BF16, name="z_woven" + name, align_bytes=64)
+            weave(
                 woven[:].rearrange("p (c i t) -> p c t i", i=4, t=PACK),
-                z_rows[u][:].rearrange("p (t c i) -> p c t i", i=4, t=PACK),
+                z_rows[u][:].rearrange("p (t c i) -> p c t i", i=4, t=PACK)[:, start // 4 : (start + width) // 4],
             )
-            z_codes = keep.tile([P, HALF_V], U32, name="z_codes%d" % u, align_bytes=64)
-            z_bytes = keep.tile([P, HALF_V], U8, name="z_bytes%d" % u, align_bytes=64)
+            z_codes = keep.tile([P, width], U32, name="z_codes" + name, align_bytes=64)
+            z_bytes = keep.tile([P, width], U8, name="z_bytes" + name, align_bytes=64)
             nc.vector.quantize_mx(out=z_codes[:].bitcast(FP8X4), scales=z_bytes[:], in_=woven[:])
-            for g in range(2):
+            blocks = PACK // len(engines)
+            for g, engine in enumerate(engines):
                 bank = psum.tile([P, BANK], F32, name="bank")
-                for b in range(2):
-                    cols = slice((2 * g + b) * P, (2 * g + b + 1) * P)
+                for b in range(blocks):
+                    cols = slice((blocks * g + b) * P, (blocks * g + b + 1) * P)
                     nc.tensor.matmul_mx(
-                        out=bank[:, b * HALF_V : (b + 1) * HALF_V],
+                        out=bank[:, b * width : (b + 1) * width],
                         lhsT=cand_codes[:, cols].bitcast(FP8X4),
                         lhsT_scale=cand_bytes[:, cols],
                         rhs=z_codes[:].bitcast(FP8X4),
@@ -170,33 +184,34 @@ def tile_picked_candwide_none_p_kernel(
                         start=True,
                         stop=True,
                     )
-                scores = keep.tile([P, BANK], F32, name="scores%d_%d" % (u, g))
-                if u == 1 and g == 1:
-                    nc.vector.tensor_scalar(scores[:], bank[:], 0.0625, None, ALU.mult)
+                scores = keep.tile([P, blocks * width], F32, name="scores%s_%d" % (name, g))
+                if engine == "vector":
+                    nc.vector.tensor_scalar(scores[:], bank[:, : blocks * width], 0.0625, None, ALU.mult)
                 else:
-                    nc.scalar.activation(scores[:], bank[:], COPY, scale=0.0625)
-                nc.sync.dma_start(
-                    out_rows[:, 2 * g : 2 * g + 2, u * HALF_V : (u + 1) * HALF_V],
-                    scores[:].rearrange("p (b v) -> p b v", b=2),
+                    nc.scalar.activation(scores[:], bank[:, : blocks * width], COPY, scale=0.0625)
+                first = u * HALF_V + start
+                queue = nc.scalar if (engine == "scalar" and u == 1 and start > 0) else nc.sync
+                queue.dma_start(
+                    out_rows[:, blocks * g : blocks * (g + 1), first : first + width],
+                    scores[:].rearrange("p (b v) -> p b v", b=blocks),
                 )
 
-        first_product(0)
-        first_product(1)
-        look_up(0, 0, True)
+        for pair in range(2):
+            for c in range(2):
+                first_product(2 * pair, c)
+                first_product(2 * pair + 1, c)
         nc.vector.tensor_copy(cand_bytes[:], byte_table[:].indirect(cand_t[:]))
-        look_up(1, 0, False)
-        first_product(2)
+        look_up(0, 0, True)
+        look_up(1, 0, True)
+        look_up(2, 0, False)
+        look_up(3, 0, False)
         contrast([0, 1], 0)
         nc.vector.tensor_copy(cand_codes[:], word_table[:].bitcast(U32).indirect(cand_t[:]))
-        look_up(2, 0, False)
-        first_product(3)
-        look_up(0, 1, True)
-        look_up(3, 0, False)
         contrast([2, 3], 0)
-        look_up(1, 1, False)
-        look_up(2, 1, False)
-        look_up(3, 1, False)
-        second_product(0)
+        for t in range(PACK):
+            look_up(t, 1, False)
+        second_product(0, 0, HALF_V, ["scalar", "scalar"], nc.vector.tensor_copy)
         contrast([0, 1], 1)
         contrast([2, 3], 1)
-        second_product(1)
+        second_product(1, 0, HALF_V // 2, ["scalar"], nc.vector.tensor_copy)
+        second_product(1, HALF_V // 2, HALF_V // 2, ["scalar", "vector"], nc.scalar.copy)

@@ -37,6 +37,7 @@ def tile_picked_candwide_none_p_kernel(
         gain = keep.tile([P, PACK], F32, name="gain")
 
         nc.gpsimd.memset(byte_table[:].bitcast(I32), 0)
+        nc.sync.dma_start(gain[:], gs.rearrange("(p t) o -> p (t o)", t=PACK))
         nc.sync.dma_start(offs_t[:], offs)
         nc.sync.dma_start(cand_t[:], cand)
         nc.sync.dma_start(order_t[:], order)
@@ -51,7 +52,15 @@ def tile_picked_candwide_none_p_kernel(
             raw = keep.tile([P, PACK, H // 2], F32, name="w_raw%d" % u)
             nc.sync.dma_start(raw[:], w_rows[:, :, u * (H // 2) : (u + 1) * (H // 2)])
             w_raw.append(raw)
-        nc.sync.dma_start(gain[:], gs.rearrange("(p t) o -> p (t o)", t=PACK))
+
+        half_gain = keep.tile([P, PACK], F32, name="half_gain")
+        positive = keep.tile([P, PACK], F32, name="positive")
+        slope = keep.tile([P, PACK], F32, name="slope")
+        weight = keep.tile([P, PACK], F32, name="weight")
+        nc.vector.tensor_scalar(positive[:], gain[:], 0.0, None, ALU.is_ge)
+        nc.vector.tensor_scalar(half_gain[:], gain[:], 0.5, None, ALU.mult)
+        nc.vector.tensor_scalar(slope[:], positive[:], 1.5, -2.0, ALU.mult, ALU.add)
+        nc.vector.tensor_scalar(weight[:], positive[:], 3.0, -1.0, ALU.mult, ALU.add)
 
         x_bytes, x_codes = [], []
         shared = ctx.enter_context(tc.tile_pool(name="shared", bufs=1))
@@ -83,15 +92,6 @@ def tile_picked_candwide_none_p_kernel(
         w_bytes = keep.tile([P, PACK * P], U8, name="w_bytes", align_bytes=64)
         nc.vector.quantize_mx(out=w_codes[:].bitcast(FP8X4), scales=w_bytes[:], in_=w_bf[:])
         pick_bytes(1)
-
-        half_gain = keep.tile([P, PACK], F32, name="half_gain")
-        positive = keep.tile([P, PACK], F32, name="positive")
-        slope = keep.tile([P, PACK], F32, name="slope")
-        weight = keep.tile([P, PACK], F32, name="weight")
-        nc.gpsimd.tensor_scalar(half_gain[:], gain[:], 0.5, None, ALU.mult)
-        nc.gpsimd.tensor_scalar(positive[:], gain[:], 0.0, None, ALU.is_ge)
-        nc.gpsimd.tensor_scalar(slope[:], positive[:], 1.5, -2.0, ALU.mult, ALU.add)
-        nc.gpsimd.tensor_scalar(weight[:], positive[:], 3.0, -1.0, ALU.mult, ALU.add)
 
         cand_bytes = shared.tile([P, C], U8, name="cand_bytes", align_bytes=64, offset=0)
         cand_codes = shared.tile([P, C], U32, name="cand_codes", align_bytes=64, offset=1024)

@@ -18,7 +18,14 @@ COPY = mybir.ActivationFunctionType.Copy
 P = 128
 PACK = 4
 BANK = 512
+BANKS = 8
+QUADRANT = 32
+ALIGN = 64
+STRIPE = 16
+HALF_S = S // 2
 HALF_V = V // 2
+PIECE = HALF_V // 2
+OUT_SCALE = 0.0625
 
 
 def tile_picked_candwide_none_p_kernel(
@@ -27,31 +34,36 @@ def tile_picked_candwide_none_p_kernel(
     nc = tc.nc
     with ExitStack() as ctx:
         keep = ctx.enter_context(tc.tile_pool(name="keep", bufs=1))
-        psum = ctx.enter_context(tc.psum_pool(name="psum", bufs=8))
+        reused = ctx.enter_context(tc.tile_pool(name="reused", bufs=1))
+        psum = ctx.enter_context(tc.psum_pool(name="psum", bufs=BANKS))
 
-        offs_t = keep.tile([P, S // 16], U16, name="offs_t")
-        order_t = keep.tile([P, S // 16], U16, name="order_t")
-        cand_t = keep.tile([P, C // 16], U16, name="cand_t")
-        word_table = keep.tile([P, T], I32, name="word_table", align_bytes=64)
-        byte_table = keep.tile([P, T], U8, name="byte_table", align_bytes=64)
+        def list_half(list_tile, half):
+            return list_tile[:, half * HALF_S // STRIPE : (half + 1) * HALF_S // STRIPE]
+
+        offs_list = keep.tile([P, S // STRIPE], U16, name="offs_list")
+        order_list = keep.tile([P, S // STRIPE], U16, name="order_list")
+        cand_list = keep.tile([P, C // STRIPE], U16, name="cand_list")
+        word_table = keep.tile([P, T], I32, name="word_table", align_bytes=ALIGN)
+        byte_table = keep.tile([P, T], U8, name="byte_table", align_bytes=ALIGN)
         gain = keep.tile([P, PACK], F32, name="gain")
 
         nc.gpsimd.memset(byte_table[:].bitcast(I32), 0)
         nc.sync.dma_start(gain[:], gs.rearrange("(p t) o -> p (t o)", t=PACK))
-        nc.sync.dma_start(offs_t[:], offs)
-        nc.sync.dma_start(cand_t[:], cand)
-        nc.sync.dma_start(order_t[:], order)
-        nc.sync.dma_start(word_table[:], x_words[0].rearrange("p n t -> p (n t)").bitcast(I32))
-        for q in range(4):
+        nc.sync.dma_start(offs_list[:], offs)
+        nc.sync.dma_start(cand_list[:], cand)
+        nc.sync.dma_start(word_table[:], x_words[0].rearrange("p n j -> p (n j)").bitcast(I32))
+        for q in range(P // QUADRANT):
             nc.scalar.dma_start(
-                byte_table[32 * q : 32 * q + 4, :].bitcast(I32), x_scales[0, 4 * q : 4 * q + 4, :].bitcast(I32)
+                byte_table[QUADRANT * q : QUADRANT * q + 4, :].bitcast(I32),
+                x_scales[0, 4 * q : 4 * q + 4, :].bitcast(I32),
             )
         w_rows = w1.rearrange("(p j) c -> p j c", j=PACK)
         w_raw = []
-        for u in range(2):
-            raw = keep.tile([P, PACK, H // 2], F32, name="w_raw%d" % u)
-            nc.sync.dma_start(raw[:], w_rows[:, :, u * (H // 2) : (u + 1) * (H // 2)])
+        for half in range(2):
+            raw = keep.tile([P, PACK, H // 2], F32, name="w_raw%d" % half)
+            nc.sync.dma_start(raw[:], w_rows[:, :, half * H // 2 : (half + 1) * H // 2])
             w_raw.append(raw)
+        nc.sync.dma_start(order_list[:], order)
 
         half_gain = keep.tile([P, PACK], F32, name="half_gain")
         positive = keep.tile([P, PACK], F32, name="positive")
@@ -62,119 +74,134 @@ def tile_picked_candwide_none_p_kernel(
         nc.vector.tensor_scalar(slope[:], positive[:], 1.5, -2.0, ALU.mult, ALU.add)
         nc.vector.tensor_scalar(weight[:], positive[:], 3.0, -1.0, ALU.mult, ALU.add)
 
-        x_bytes, x_codes = [], []
-        shared = ctx.enter_context(tc.tile_pool(name="shared", bufs=1))
+        def gather_words(picked, offsets):
+            nc.vector.tensor_copy(picked[:], word_table[:].bitcast(U32).indirect(offsets))
 
-        def pick_bytes(c):
-            if c == 0:
-                picked = keep.tile([P, BANK], U8, name="x_bytes0", align_bytes=64)
-            else:
-                picked = shared.tile([P, BANK], U8, name="x_bytes1", align_bytes=64, offset=512)
-            nc.vector.tensor_copy(picked[:], byte_table[:].indirect(offs_t[:, 32 * c : 32 * c + 32]))
-            x_bytes.append(picked)
+        def gather_bytes(picked, offsets):
+            nc.vector.tensor_copy(picked[:], byte_table[:].indirect(offsets))
 
-        def pick_words(c):
-            picked = keep.tile([P, BANK], U32, name="x_codes%d" % c, align_bytes=64)
-            nc.vector.tensor_copy(picked[:], word_table[:].bitcast(U32).indirect(offs_t[:, 32 * c : 32 * c + 32]))
-            x_codes.append(picked)
+        x_codes = [keep.tile([P, HALF_S], U32, name="x_codes%d" % half, align_bytes=ALIGN) for half in range(2)]
+        first_bytes = keep.tile([P, HALF_S], U8, name="first_bytes", align_bytes=ALIGN)
+        gather_words(x_codes[0], list_half(offs_list, 0))
+        gather_words(x_codes[1], list_half(offs_list, 1))
+        gather_bytes(first_bytes, list_half(offs_list, 0))
 
-        pick_words(0)
-        pick_words(1)
-        pick_bytes(0)
+        rounded_bytes = 2 * P * PACK * 2
+        w_rounded = [
+            reused.tile([P, 2 * P * PACK], BF16, name="w_rounded%d" % n, align_bytes=ALIGN, offset=n * rounded_bytes)
+            for n in range(2)
+        ]
+        for half in range(2):
+            for n in range(2):
+                nc.scalar.copy(
+                    w_rounded[n][:].rearrange("p (t m j) -> p m j t", t=2, j=PACK)[:, half * P // 2 : (half + 1) * P // 2],
+                    w_raw[half][:].rearrange("p j (m t) -> p m j t", t=PACK)[:, :, :, 2 * n : 2 * n + 2],
+                )
+        w_codes = keep.tile([P, H], U32, name="w_codes", align_bytes=ALIGN)
+        w_bytes = keep.tile([P, H], U8, name="w_bytes", align_bytes=ALIGN)
 
-        w_bf = shared.tile([P, PACK * P * PACK], BF16, name="w_bf", align_bytes=64, offset=0)
-        w_bf_view = w_bf[:].rearrange("p (t m j) -> p m j t", t=PACK, j=PACK)
-        for u in range(2):
-            nc.scalar.copy(
-                w_bf_view[:, 64 * u : 64 * u + 64], w_raw[u][:].rearrange("p j (m t) -> p m j t", t=PACK)
-            )
-        w_codes = keep.tile([P, PACK * P], U32, name="w_codes", align_bytes=64)
-        w_bytes = keep.tile([P, PACK * P], U8, name="w_bytes", align_bytes=64)
-        nc.vector.quantize_mx(out=w_codes[:].bitcast(FP8X4), scales=w_bytes[:], in_=w_bf[:])
-        pick_bytes(1)
+        def quantise_weights(n):
+            cols = slice(2 * P * n, 2 * P * (n + 1))
+            nc.vector.quantize_mx(out=w_codes[:, cols].bitcast(FP8X4), scales=w_bytes[:, cols], in_=w_rounded[n][:])
 
-        cand_bytes = shared.tile([P, C], U8, name="cand_bytes", align_bytes=64, offset=0)
-        cand_codes = shared.tile([P, C], U32, name="cand_codes", align_bytes=64, offset=1024)
+        quantise_weights(0)
+        second_bytes = reused.tile([P, HALF_S], U8, name="second_bytes", align_bytes=ALIGN, offset=C)
+        gather_bytes(second_bytes, list_half(offs_list, 1))
+        quantise_weights(1)
+        x_bytes = [first_bytes, second_bytes]
+        cand_bytes = reused.tile([P, C], U8, name="cand_bytes", align_bytes=ALIGN, offset=0)
+        cand_codes = reused.tile([P, C], U32, name="cand_codes", align_bytes=ALIGN, offset=rounded_bytes)
 
-        h_rows = [keep.tile([P, S], F32, name="h_rows%d" % t) for t in range(PACK)]
+        g_rows = [keep.tile([P, S], F32, name="g_rows%d" % t) for t in range(PACK)]
 
-        def first_product(t, c):
+        def first_product(t, half):
             cols = slice(t * P, (t + 1) * P)
             bank = psum.tile([P, BANK], F32, name="bank")
             nc.tensor.matmul_mx(
                 out=bank[:],
                 lhsT=w_codes[:, cols].bitcast(FP8X4),
                 lhsT_scale=w_bytes[:, cols],
-                rhs=x_codes[c][:].bitcast(FP8X4),
-                rhs_scale=x_bytes[c][:],
+                rhs=x_codes[half][:].bitcast(FP8X4),
+                rhs_scale=x_bytes[half][:],
                 start=True,
                 stop=True,
             )
-            if (t, c) == (3, 1):
-                nc.vector.tensor_scalar(
-                    h_rows[t][:, c * BANK : (c + 1) * BANK], bank[:], half_gain[:, t : t + 1], None, ALU.mult
-                )
+            target = g_rows[t][:, half * HALF_S : (half + 1) * HALF_S]
+            if (t, half) == (PACK - 1, 1):
+                nc.vector.tensor_scalar(target, bank[:], half_gain[:, t : t + 1], None, ALU.mult)
             else:
-                nc.scalar.activation(
-                    h_rows[t][:, c * BANK : (c + 1) * BANK], bank[:], COPY, scale=half_gain[:, t : t + 1]
-                )
+                nc.scalar.activation(target, bank[:], COPY, scale=half_gain[:, t : t + 1])
 
-        lined, pair_tiles = {}, {}
+        for n in range(2):
+            for half in range(2):
+                first_product(2 * n, half)
+                first_product(2 * n + 1, half)
+        gather_bytes(cand_bytes, cand_list[:])
 
-        def look_up(t, u, on_vector):
-            if t % 2 == 0:
-                pair_tiles[t // 2, u] = keep.tile([P, 4 * HALF_V], F32, name="lined%d_%d" % (t, u))
-            got = pair_tiles[t // 2, u][:, (t % 2) * 2 * HALF_V : (t % 2 + 1) * 2 * HALF_V]
-            window = h_rows[t][:].indirect(order_t[:, 32 * u : 32 * u + 32])
-            if on_vector:
-                nc.vector.tensor_copy(got, window)
-            else:
-                nc.scalar.activation(got, window, COPY)
-            lined[t, u] = got
+        pairs = {}
+        for half in range(2):
+            for t in range(PACK):
+                lined = keep.tile([P, HALF_S], F32, name="lined%d_%d" % (t, half))
+                looked_up = g_rows[t][:].indirect(list_half(order_list, half))
+                if half == 0 and t < 2:
+                    nc.vector.tensor_copy(lined[:], looked_up)
+                else:
+                    nc.scalar.activation(lined[:], looked_up, COPY)
+                pairs[t, half] = lined[:].rearrange("p (v two) -> p v two", two=2)
+        gather_words(cand_codes, cand_list[:])
 
-        z_rows = [keep.tile([P, PACK * HALF_V], BF16, name="z_rows%d" % u) for u in range(2)]
+        widths = (HALF_V, PIECE)
+        z_rows = [keep.tile([P, PACK * HALF_V], BF16, name="z_rows%d" % half) for half in range(2)]
+        z_woven = [keep.tile([P, HALF_V * PACK], BF16, name="z_woven%d" % half, align_bytes=ALIGN) for half in range(2)]
+        diff, bent = {}, {}
 
-        def contrast(ts, u):
-            diff, bent = {}, {}
-            both = keep.tile([P, len(ts) * HALF_V], F32, name="diff%d_%d" % (ts[0], u))
-            source = lined[ts[0], u] if len(ts) == 1 else pair_tiles[ts[0] // 2, u][:]
-            pairs = source.rearrange("p (v two) -> p v two", two=2)
-            nc.vector.tensor_tensor(both[:], pairs[:, :, 0], pairs[:, :, 1], ALU.subtract)
-            for n, t in enumerate(ts):
-                diff[t] = both[:, n * HALF_V : (n + 1) * HALF_V]
-            for t in ts:
-                bent[t] = keep.tile([P, HALF_V], F32, name="bent%d_%d" % (t, u))
-                nc.vector.scalar_tensor_tensor(
-                    bent[t][:], diff[t], slope[:, t : t + 1], diff[t], ALU.mult, ALU.max
-                )
-            for t in ts:
-                pairs = lined[t, u].rearrange("p (v two) -> p v two", two=2)
-                nc.vector.scalar_tensor_tensor(
-                    z_rows[u][:, t * HALF_V : (t + 1) * HALF_V],
-                    bent[t][:],
-                    weight[:, t : t + 1],
-                    pairs[:, :, 1],
-                    ALU.mult,
-                    ALU.add,
-                )
+        def subtract(t, half):
+            diff[t, half] = keep.tile([P, HALF_V], F32, name="diff%d_%d" % (t, half))
+            nc.vector.tensor_tensor(diff[t, half][:], pairs[t, half][:, :, 0], pairs[t, half][:, :, 1], ALU.subtract)
 
-        out_rows = out.rearrange("(b p) v -> p b v", p=P)
-
-        def second_product(u, start, width, engines, weave):
-            name = "%d_%d" % (u, start)
-            woven = keep.tile([P, width * PACK], BF16, name="z_woven" + name, align_bytes=64)
-            weave(
-                woven[:].rearrange("p (c i t) -> p c t i", i=4, t=PACK),
-                z_rows[u][:].rearrange("p (t c i) -> p c t i", i=4, t=PACK)[:, start // 4 : (start + width) // 4],
+        def bend(t, half):
+            bent[t, half] = keep.tile([P, HALF_V], F32, name="bent%d_%d" % (t, half))
+            nc.vector.scalar_tensor_tensor(
+                bent[t, half][:], diff[t, half][:], slope[:, t : t + 1], diff[t, half][:], ALU.mult, ALU.max
             )
-            z_codes = keep.tile([P, width], U32, name="z_codes" + name, align_bytes=64)
-            z_bytes = keep.tile([P, width], U8, name="z_bytes" + name, align_bytes=64)
-            nc.vector.quantize_mx(out=z_codes[:].bitcast(FP8X4), scales=z_bytes[:], in_=woven[:])
-            blocks = PACK // len(engines)
-            for g, engine in enumerate(engines):
+
+        def finish(t, half, pieces=slice(None)):
+            width = widths[half]
+            nc.vector.scalar_tensor_tensor(
+                z_rows[half][:].rearrange("p (n t v) -> p t n v", t=PACK, v=width)[:, t, pieces],
+                bent[t, half][:].rearrange("p (n v) -> p n v", v=width)[:, pieces],
+                weight[:, t : t + 1],
+                pairs[t, half][:, :, 1].rearrange("p (n v) -> p n v", v=width)[:, pieces],
+                ALU.mult,
+                ALU.add,
+            )
+
+        def piece_span(half, piece):
+            return slice(piece * widths[half] * PACK, (piece + 1) * widths[half] * PACK)
+
+        def weave(half, piece):
+            span = piece_span(half, piece)
+            nc.vector.tensor_copy(
+                z_woven[half][:, span].rearrange("p (c i t) -> p c t i", i=4, t=PACK),
+                z_rows[half][:, span].rearrange("p (t c i) -> p c t i", i=4, t=PACK),
+            )
+
+        out_blocks = out.rearrange("(b p) v -> p b v", p=P)
+
+        def second_product(half, piece, readers):
+            width = widths[half]
+            name = "%d_%d" % (half, piece)
+            z_codes = keep.tile([P, width], U32, name="z_codes" + name, align_bytes=ALIGN)
+            z_bytes = keep.tile([P, width], U8, name="z_bytes" + name, align_bytes=ALIGN)
+            nc.vector.quantize_mx(
+                out=z_codes[:].bitcast(FP8X4), scales=z_bytes[:], in_=z_woven[half][:, piece_span(half, piece)]
+            )
+            blocks = C // P // len(readers)
+            first_column = half * HALF_V + piece * width
+            for n, (engine, queue) in enumerate(readers):
                 bank = psum.tile([P, BANK], F32, name="bank")
                 for b in range(blocks):
-                    cols = slice((blocks * g + b) * P, (blocks * g + b + 1) * P)
+                    cols = slice((blocks * n + b) * P, (blocks * n + b + 1) * P)
                     nc.tensor.matmul_mx(
                         out=bank[:, b * width : (b + 1) * width],
                         lhsT=cand_codes[:, cols].bitcast(FP8X4),
@@ -184,34 +211,38 @@ def tile_picked_candwide_none_p_kernel(
                         start=True,
                         stop=True,
                     )
-                scores = keep.tile([P, blocks * width], F32, name="scores%s_%d" % (name, g))
+                scores = keep.tile([P, blocks * width], F32, name="scores%s_%d" % (name, n))
                 if engine == "vector":
-                    nc.vector.tensor_scalar(scores[:], bank[:, : blocks * width], 0.0625, None, ALU.mult)
+                    nc.vector.tensor_scalar(scores[:], bank[:, : blocks * width], OUT_SCALE, None, ALU.mult)
                 else:
-                    nc.scalar.activation(scores[:], bank[:, : blocks * width], COPY, scale=0.0625)
-                first = u * HALF_V + start
-                queue = nc.scalar if (engine == "scalar" and u == 1 and start > 0) else nc.sync
+                    nc.scalar.activation(scores[:], bank[:, : blocks * width], COPY, scale=OUT_SCALE)
                 queue.dma_start(
-                    out_rows[:, blocks * g : blocks * (g + 1), first : first + width],
+                    out_blocks[:, blocks * n : blocks * (n + 1), first_column : first_column + width],
                     scores[:].rearrange("p (b v) -> p b v", b=blocks),
                 )
 
-        for pair in range(2):
-            for c in range(2):
-                first_product(2 * pair, c)
-                first_product(2 * pair + 1, c)
-        nc.vector.tensor_copy(cand_bytes[:], byte_table[:].indirect(cand_t[:]))
-        look_up(0, 0, True)
-        look_up(1, 0, True)
-        look_up(2, 0, False)
-        look_up(3, 0, False)
-        contrast([0, 1], 0)
-        nc.vector.tensor_copy(cand_codes[:], word_table[:].bitcast(U32).indirect(cand_t[:]))
-        contrast([2, 3], 0)
-        for t in range(PACK):
-            look_up(t, 1, False)
-        second_product(0, 0, HALF_V, ["scalar", "scalar"], nc.vector.tensor_copy)
-        contrast([0, 1], 1)
-        contrast([2, 3], 1)
-        second_product(1, 0, HALF_V // 2, ["scalar"], nc.vector.tensor_copy)
-        second_product(1, HALF_V // 2, HALF_V // 2, ["scalar", "vector"], nc.scalar.copy)
+        for tiles in ((0, 1), (2, 3)):
+            for step in (subtract, bend, finish):
+                for t in tiles:
+                    step(t, 0)
+
+        subtract(0, 1)
+        weave(0, 0)
+        subtract(1, 1)
+        second_product(0, 0, [("scalar", nc.sync), ("scalar", nc.sync)])
+        for step in (bend, finish):
+            for t in (0, 1):
+                step(t, 1)
+        for step in (subtract, bend):
+            for t in (2, 3):
+                step(t, 1)
+
+        first_piece, last_piece = slice(0, 1), slice(1, 2)
+        finish(2, 1, first_piece)
+        finish(3, 1, first_piece)
+        finish(2, 1, last_piece)
+        weave(1, 0)
+        finish(3, 1, last_piece)
+        second_product(1, 0, [("scalar", nc.sync)])
+        weave(1, 1)
+        second_product(1, 1, [("scalar", nc.scalar), ("vector", nc.sync)])

from contextlib import ExitStack

import concourse.mybir as mybir

K, T, S, V, H, C = 512, 2048, 1024, 512, 512, 512
FLOPS = 2 * K * H * S + 2 * K * C * V

F32 = mybir.dt.float32
BF16 = mybir.dt.bfloat16
I32 = mybir.dt.int32
U32 = mybir.dt.uint32
U16 = mybir.dt.uint16
U8 = mybir.dt.uint8
FP8X4 = mybir.dt.float8_e4m3fn_x4
ALU = mybir.AluOpType
COPY = mybir.ActivationFunctionType.Copy

P = 128
PACK = 4
BANK = 512
BANKS = 8
QUADRANT = 32
ALIGN = 64
STRIPE = 16
HALF_S = S // 2
HALF_V = V // 2
PIECE = HALF_V // 2
OUT_SCALE = 0.0625


def tile_picked_candwide_none_p_kernel(
    tc, x_words, x_scales, w1, gs, offs, order, cand, out
):
    nc = tc.nc
    with ExitStack() as ctx:
        keep = ctx.enter_context(tc.tile_pool(name="keep", bufs=1))
        reused = ctx.enter_context(tc.tile_pool(name="reused", bufs=1))
        psum = ctx.enter_context(tc.psum_pool(name="psum", bufs=BANKS))

        def list_half(list_tile, half):
            return list_tile[:, half * HALF_S // STRIPE : (half + 1) * HALF_S // STRIPE]

        offs_list = keep.tile([P, S // STRIPE], U16, name="offs_list")
        order_list = keep.tile([P, S // STRIPE], U16, name="order_list")
        cand_list = keep.tile([P, C // STRIPE], U16, name="cand_list")
        word_table = keep.tile([P, T], I32, name="word_table", align_bytes=ALIGN)
        byte_table = keep.tile([P, T], U8, name="byte_table", align_bytes=ALIGN)
        gain = keep.tile([P, PACK], F32, name="gain")

        nc.gpsimd.memset(byte_table[:].bitcast(I32), 0)
        nc.sync.dma_start(gain[:], gs.rearrange("(p t) o -> p (t o)", t=PACK))
        nc.sync.dma_start(offs_list[:], offs)
        nc.sync.dma_start(cand_list[:], cand)
        nc.sync.dma_start(word_table[:], x_words[0].rearrange("p n j -> p (n j)").bitcast(I32))
        for q in range(P // QUADRANT):
            nc.scalar.dma_start(
                byte_table[QUADRANT * q : QUADRANT * q + 4, :].bitcast(I32),
                x_scales[0, 4 * q : 4 * q + 4, :].bitcast(I32),
            )
        w_rows = w1.rearrange("(p j) c -> p j c", j=PACK)
        w_raw = []
        for half in range(2):
            raw = keep.tile([P, PACK, H // 2], F32, name="w_raw%d" % half)
            nc.sync.dma_start(raw[:], w_rows[:, :, half * H // 2 : (half + 1) * H // 2])
            w_raw.append(raw)
        nc.sync.dma_start(order_list[:], order)

        half_gain = keep.tile([P, PACK], F32, name="half_gain")
        positive = keep.tile([P, PACK], F32, name="positive")
        slope = keep.tile([P, PACK], F32, name="slope")
        weight = keep.tile([P, PACK], F32, name="weight")
        nc.vector.tensor_scalar(positive[:], gain[:], 0.0, None, ALU.is_ge)
        nc.vector.tensor_scalar(half_gain[:], gain[:], 0.5, None, ALU.mult)
        nc.vector.tensor_scalar(slope[:], positive[:], 1.5, -2.0, ALU.mult, ALU.add)
        nc.vector.tensor_scalar(weight[:], positive[:], 3.0, -1.0, ALU.mult, ALU.add)

        def gather_words(picked, offsets):
            nc.vector.tensor_copy(picked[:], word_table[:].bitcast(U32).indirect(offsets))

        def gather_bytes(picked, offsets):
            nc.vector.tensor_copy(picked[:], byte_table[:].indirect(offsets))

        x_codes = [keep.tile([P, HALF_S], U32, name="x_codes%d" % half, align_bytes=ALIGN) for half in range(2)]
        first_bytes = keep.tile([P, HALF_S], U8, name="first_bytes", align_bytes=ALIGN)
        gather_words(x_codes[0], list_half(offs_list, 0))
        gather_words(x_codes[1], list_half(offs_list, 1))
        gather_bytes(first_bytes, list_half(offs_list, 0))

        rounded_bytes = 2 * P * PACK * 2
        w_rounded = [
            reused.tile([P, 2 * P * PACK], BF16, name="w_rounded%d" % n, align_bytes=ALIGN, offset=n * rounded_bytes)
            for n in range(2)
        ]
        for half in range(2):
            for n in range(2):
                nc.scalar.copy(
                    w_rounded[n][:].rearrange("p (t m j) -> p m j t", t=2, j=PACK)[:, half * P // 2 : (half + 1) * P // 2],
                    w_raw[half][:].rearrange("p j (m t) -> p m j t", t=PACK)[:, :, :, 2 * n : 2 * n + 2],
                )
        w_codes = keep.tile([P, H], U32, name="w_codes", align_bytes=ALIGN)
        w_bytes = keep.tile([P, H], U8, name="w_bytes", align_bytes=ALIGN)

        def quantise_weights(n):
            cols = slice(2 * P * n, 2 * P * (n + 1))
            nc.vector.quantize_mx(out=w_codes[:, cols].bitcast(FP8X4), scales=w_bytes[:, cols], in_=w_rounded[n][:])

        quantise_weights(0)
        second_bytes = reused.tile([P, HALF_S], U8, name="second_bytes", align_bytes=ALIGN, offset=C)
        gather_bytes(second_bytes, list_half(offs_list, 1))
        quantise_weights(1)
        x_bytes = [first_bytes, second_bytes]
        cand_bytes = reused.tile([P, C], U8, name="cand_bytes", align_bytes=ALIGN, offset=0)
        cand_codes = reused.tile([P, C], U32, name="cand_codes", align_bytes=ALIGN, offset=rounded_bytes)

        g_rows = [keep.tile([P, S], F32, name="g_rows%d" % t) for t in range(PACK)]

        def first_product(t, half):
            cols = slice(t * P, (t + 1) * P)
            bank = psum.tile([P, BANK], F32, name="bank")
            nc.tensor.matmul_mx(
                out=bank[:],
                lhsT=w_codes[:, cols].bitcast(FP8X4),
                lhsT_scale=w_bytes[:, cols],
                rhs=x_codes[half][:].bitcast(FP8X4),
                rhs_scale=x_bytes[half][:],
                start=True,
                stop=True,
            )
            target = g_rows[t][:, half * HALF_S : (half + 1) * HALF_S]
            if (t, half) == (PACK - 1, 1):
                nc.vector.tensor_scalar(target, bank[:], half_gain[:, t : t + 1], None, ALU.mult)
            else:
                nc.scalar.activation(target, bank[:], COPY, scale=half_gain[:, t : t + 1])

        for n in range(2):
            for half in range(2):
                first_product(2 * n, half)
                first_product(2 * n + 1, half)
        gather_bytes(cand_bytes, cand_list[:])

        pairs = {}
        for half in range(2):
            for t in range(PACK):
                lined = keep.tile([P, HALF_S], F32, name="lined%d_%d" % (t, half))
                looked_up = g_rows[t][:].indirect(list_half(order_list, half))
                if half == 0 and t < 2:
                    nc.vector.tensor_copy(lined[:], looked_up)
                else:
                    nc.scalar.activation(lined[:], looked_up, COPY)
                pairs[t, half] = lined[:].rearrange("p (v two) -> p v two", two=2)
        gather_words(cand_codes, cand_list[:])

        widths = (HALF_V, PIECE)
        z_rows = [keep.tile([P, PACK * HALF_V], BF16, name="z_rows%d" % half) for half in range(2)]
        z_woven = [keep.tile([P, HALF_V * PACK], BF16, name="z_woven%d" % half, align_bytes=ALIGN) for half in range(2)]
        diff, bent = {}, {}

        def subtract(t, half):
            diff[t, half] = keep.tile([P, HALF_V], F32, name="diff%d_%d" % (t, half))
            nc.vector.tensor_tensor(diff[t, half][:], pairs[t, half][:, :, 0], pairs[t, half][:, :, 1], ALU.subtract)

        def bend(t, half):
            bent[t, half] = keep.tile([P, HALF_V], F32, name="bent%d_%d" % (t, half))
            nc.vector.scalar_tensor_tensor(
                bent[t, half][:], diff[t, half][:], slope[:, t : t + 1], diff[t, half][:], ALU.mult, ALU.max
            )

        def finish(t, half, pieces=slice(None)):
            width = widths[half]
            nc.vector.scalar_tensor_tensor(
                z_rows[half][:].rearrange("p (n t v) -> p t n v", t=PACK, v=width)[:, t, pieces],
                bent[t, half][:].rearrange("p (n v) -> p n v", v=width)[:, pieces],
                weight[:, t : t + 1],
                pairs[t, half][:, :, 1].rearrange("p (n v) -> p n v", v=width)[:, pieces],
                ALU.mult,
                ALU.add,
            )

        def piece_span(half, piece):
            return slice(piece * widths[half] * PACK, (piece + 1) * widths[half] * PACK)

        def weave(half, piece):
            span = piece_span(half, piece)
            nc.vector.tensor_copy(
                z_woven[half][:, span].rearrange("p (c i t) -> p c t i", i=4, t=PACK),
                z_rows[half][:, span].rearrange("p (t c i) -> p c t i", i=4, t=PACK),
            )

        out_blocks = out.rearrange("(b p) v -> p b v", p=P)

        def second_product(half, piece, readers):
            width = widths[half]
            name = "%d_%d" % (half, piece)
            z_codes = keep.tile([P, width], U32, name="z_codes" + name, align_bytes=ALIGN)
            z_bytes = keep.tile([P, width], U8, name="z_bytes" + name, align_bytes=ALIGN)
            nc.vector.quantize_mx(
                out=z_codes[:].bitcast(FP8X4), scales=z_bytes[:], in_=z_woven[half][:, piece_span(half, piece)]
            )
            blocks = C // P // len(readers)
            first_column = half * HALF_V + piece * width
            for n, (engine, queue) in enumerate(readers):
                bank = psum.tile([P, BANK], F32, name="bank")
                for b in range(blocks):
                    cols = slice((blocks * n + b) * P, (blocks * n + b + 1) * P)
                    nc.tensor.matmul_mx(
                        out=bank[:, b * width : (b + 1) * width],
                        lhsT=cand_codes[:, cols].bitcast(FP8X4),
                        lhsT_scale=cand_bytes[:, cols],
                        rhs=z_codes[:].bitcast(FP8X4),
                        rhs_scale=z_bytes[:],
                        start=True,
                        stop=True,
                    )
                scores = keep.tile([P, blocks * width], F32, name="scores%s_%d" % (name, n))
                if engine == "vector":
                    nc.vector.tensor_scalar(scores[:], bank[:, : blocks * width], OUT_SCALE, None, ALU.mult)
                else:
                    nc.scalar.activation(scores[:], bank[:, : blocks * width], COPY, scale=OUT_SCALE)
                queue.dma_start(
                    out_blocks[:, blocks * n : blocks * (n + 1), first_column : first_column + width],
                    scores[:].rearrange("p (b v) -> p b v", b=blocks),
                )

        for tiles in ((0, 1), (2, 3)):
            for step in (subtract, bend, finish):
                for t in tiles:
                    step(t, 0)

        subtract(0, 1)
        weave(0, 0)
        subtract(1, 1)
        second_product(0, 0, [("scalar", nc.sync), ("scalar", nc.sync)])
        for step in (bend, finish):
            for t in (0, 1):
                step(t, 1)
        for step in (subtract, bend):
            for t in (2, 3):
                step(t, 1)

        first_piece, last_piece = slice(0, 1), slice(1, 2)
        finish(2, 1, first_piece)
        finish(3, 1, first_piece)
        finish(2, 1, last_piece)
        weave(1, 0)
        finish(3, 1, last_piece)
        second_product(1, 0, [("scalar", nc.sync)])
        weave(1, 1)
        second_product(1, 1, [("scalar", nc.scalar), ("vector", nc.sync)])
